import numpy as np
import ml_dtypes


def mxq(x, axis, fmt="e4m3"):
    dtype, down = {"e4m3": (ml_dtypes.float8_e4m3fn, 7), "e5m2": (ml_dtypes.float8_e5m2, 14)}[fmt]
    v = np.moveaxis(np.asarray(x, np.float32).astype(ml_dtypes.bfloat16).astype(np.float64), axis, -1)
    blocks = v.reshape(v.shape[:-1] + (-1, 32))
    amax = np.abs(blocks).max(-1, keepdims=True)
    byte = np.maximum(np.where(amax > 0, np.frexp(amax)[1] - 1 + 127, 0) - down, 1)
    scale = np.exp2(byte - 127.0)
    codes = (blocks / scale).astype(np.float32).astype(dtype).astype(np.float64)
    return np.moveaxis((codes * scale).reshape(v.shape), -1, axis)


WIDE = False


def mx_kscale(k):
    if not WIDE:
        return np.ones(k)
    levels = np.array([10, -10, 5, -5, 0])
    if k % 512:
        return np.exp2(np.random.permutation(np.resize(levels, k // 32))).repeat(32)
    a = np.empty((k // 512, 16))
    for p in range(k // 512):
        a[p, :8] = np.random.permutation(np.resize(levels, 8))
        for g in range(8):
            far = levels[np.abs(levels - a[p, g]) >= 10]
            a[p, g + 8] = far[np.random.randint(len(far))]
    return np.exp2(a.ravel()).repeat(32)


def f64(x):
    return np.asarray(x).astype(np.float64)


def striped(idx):
    return np.tile(idx.reshape(-1, 16).T, (8, 1)).astype(np.uint16)


def unstriped(offs):
    return offs[:16].T.reshape(-1).astype(np.int64)


E2M1 = np.array([0.0, 0.5, 1.0, 1.5, 2.0, 3.0, 4.0, 6.0, -0.0, -0.5, -1.0, -1.5, -2.0, -3.0, -4.0, -6.0])


def pack_weight(w, fmt):
    k, n = w.shape
    w = f64(np.asarray(w, np.float32).astype(ml_dtypes.bfloat16)).reshape(k // 32, 32, n)
    amax = np.abs(w).max(1)
    if fmt == "e4m3":
        byte = np.frexp(amax)[1] - 1 + 127 - 7
    else:
        mant, ex = np.frexp(amax / 6.0)
        byte = np.where(mant > 0.5, ex, ex - 1) + 127
    byte = np.clip(np.where(amax > 0, byte, 1), 1, 254)
    scaled = (w * np.exp2(127.0 - byte)[:, None, :]).reshape(k, n).astype(np.float32)
    by_word = np.ascontiguousarray(scaled.reshape(k // 512, 128, 4, n).transpose(0, 1, 3, 2))
    if fmt == "e4m3":
        words = by_word.astype(ml_dtypes.float8_e4m3fn).view(np.uint8)
    else:
        c = by_word.astype(ml_dtypes.float4_e2m1fn).view(np.uint8) & 0xF
        words = (c[..., 0::2] | (c[..., 1::2] << 4)).reshape(k // 512, 128, 2 * n)
    return np.ascontiguousarray(words), np.ascontiguousarray(byte.astype(np.uint8).reshape(k // 512, 16, n))


def unpack_weight(words, scales, fmt):
    g, _, n = scales.shape
    words = np.ascontiguousarray(words).reshape(g, 128, n, -1)
    if fmt == "e4m3":
        vals = words.view(ml_dtypes.float8_e4m3fn).astype(np.float64)
    else:
        nib = np.empty((g, 128, n, 4), np.uint8)
        nib[..., 0::2] = words & 0xF
        nib[..., 1::2] = words >> 4
        vals = E2M1[nib]
    vals = vals * np.repeat(np.exp2(scales.astype(np.float64) - 127.0), 8, axis=1)[..., None]
    return vals.transpose(0, 1, 3, 2).reshape(g * 512, n)


G, K, M, T, S = 2, 1024, 256, 1024, 256


def setup_inputs():
    n = np.random.standard_normal
    s = mx_kscale(K)[:, None]
    p_w4 = pack_weight(n((K, M)) / np.sqrt(K) / s, "e2m1")
    p_w8 = pack_weight(n((K, M)) / np.sqrt(K) / s, "e4m3")
    return {
        "xT": (n((K, T)) * s).astype(np.float32),
        "c": (n((K, S)) * s).astype(np.float32),
        "w4_words": p_w4[0],
        "w4_scales": p_w4[1],
        "w8_words": p_w8[0],
        "w8_scales": p_w8[1],
        "b": (0.3 * n(256)).astype(np.float32),
        "offs": striped(np.concatenate([np.random.permutation(T)[:S] for _ in range(G)])),
    }


def reference(xT, c, w4_words, w4_scales, w8_words, w8_scales, b, offs):
    idx = unstriped(offs).reshape(G, S)
    d_ = [mxq(f64(xT)[:, idx[g]] - f64(c), 0, "e4m3") for g in range(G)]
    c_ = mxq(f64(c), 0, "e4m3")
    w4_ = unpack_weight(w4_words, w4_scales, "e2m1")
    w8_ = unpack_weight(w8_words, w8_scales, "e4m3")
    y = np.max([(w4_.T @ d) for d in d_], axis=0) + (w8_.T @ c_)
    return y + f64(b)[:, None]

@@ -1,0 +1,169 @@
+from contextlib import ExitStack
+
+import concourse.mybir as mybir
+
+G, K, M, T, S = 2, 1024, 256, 1024, 256
+FLOPS = 2 * K * M * S * (G + 1)
+
+F32 = mybir.dt.float32
+BF16 = mybir.dt.bfloat16
+I32 = mybir.dt.int32
+U32 = mybir.dt.uint32
+U16 = mybir.dt.uint16
+U8 = mybir.dt.uint8
+FP8X4 = mybir.dt.float8_e4m3fn_x4
+FP4X4 = mybir.dt.float4_e2m1fn_x4
+ALU = mybir.AluOpType
+
+P = 128
+PACK = 4
+KP = P * PACK
+PASSES = K // KP
+MT = M // P
+H = 128
+HALVES = S // H
+
+
+def tile_list_edge_bias_kernel(tc, xT, c, w4_words, w4_scales, w8_words, w8_scales, b, offs, out):
+    nc = tc.nc
+    with ExitStack() as ctx:
+        keep = ctx.enter_context(tc.tile_pool(name="keep", bufs=1))
+        psum = ctx.enter_context(tc.psum_pool(name="psum", bufs=1))
+
+        offsets = keep.tile([P, G * S // 16], U16, name="offsets")
+        nc.sync.dma_start(offsets[:], offs)
+
+        x_rows = xT.rearrange("(a p i) t -> a i p t", p=P, i=PACK)
+        c_rows = c.rearrange("(a p i) j -> a p i j", p=P, i=PACK)
+        xs = [[keep.tile([P, T], F32, name="x%d%d" % (a, i)) for i in range(PACK)] for a in range(PASSES)]
+        cs = [keep.tile([P, PACK, S], F32, name="c%d" % a) for a in range(PASSES)]
+        w4 = keep.tile([P, PASSES, 2 * M], U8, name="w4", align_bytes=64)
+        w8 = keep.tile([P, PASSES, 4 * M], U8, name="w8", align_bytes=64)
+        s4 = keep.tile([P, PASSES, M], U8, name="s4", align_bytes=64)
+        s8 = keep.tile([P, PASSES, M], U8, name="s8", align_bytes=64)
+        bias = keep.tile([P, MT], F32, name="bias")
+
+        nc.sync.dma_start(cs[0][:, 0:1, :], c_rows[0][:, 0:1, :])
+        nc.sync.dma_start(xs[0][0][:], x_rows[0][0])
+        nc.sync.dma_start(cs[0][:, 1:PACK, :], c_rows[0][:, 1:PACK, :])
+        for i in range(1, PACK):
+            nc.sync.dma_start(xs[0][i][:], x_rows[0][i])
+        nc.sync.dma_start(cs[1][:], c_rows[1])
+        nc.sync.dma_start(w4[:].bitcast(I32), w4_words.rearrange("a p n -> p a n").bitcast(I32))
+        for i in range(PACK):
+            nc.sync.dma_start(xs[1][i][:], x_rows[1][i])
+        nc.sync.dma_start(w8[:].bitcast(I32), w8_words.rearrange("a p n i -> p a (n i)").bitcast(I32))
+        with nc.allow_non_contiguous_dma(reason="one bias value a partition"):
+            nc.sync.dma_start(bias[:], b.rearrange("(m p) -> p m", p=P))
+
+        for plane, src in ((s4, w4_scales), (s8, w8_scales)):
+            nc.gpsimd.memset(plane[:].bitcast(I32), 0)
+        for plane, src in ((s4, w4_scales), (s8, w8_scales)):
+            for q in range(4):
+                nc.gpsimd.dma_start(
+                    plane[32 * q : 32 * q + 4].bitcast(I32),
+                    src[:, 4 * q : 4 * q + 4, :].rearrange("a r n -> r a n").bitcast(I32),
+                )
+
+        def gather(dst, a, i, g, j0, n):
+            lo = (g * S + j0) // 16
+            nc.vector.tensor_tensor(dst, xs[a][i][:].indirect(offsets[:, lo : lo + n // 16]), cs[a][:, i, j0 : j0 + n], ALU.subtract)
+
+        def weave4(name, src, n):
+            woven = keep.tile([P, n, PACK], BF16, name=name, align_bytes=64)
+            nc.scalar.copy(
+                woven[:].rearrange("p (c e) t -> p c t e", e=4),
+                src.rearrange("p t (c e) -> p c t e", e=4),
+            )
+            return woven
+
+        def quantise(name, woven, n):
+            codes = keep.tile([P, n], U32, name=name + "q", align_bytes=64)
+            scales = keep.tile([P, n], U8, name=name + "s", align_bytes=64)
+            nc.vector.quantize_mx(codes[:].bitcast(FP8X4), scales[:], woven[:].rearrange("p j t -> p (j t)"))
+            return codes, scales
+
+        edge = [[psum.tile([P, 512], F32, name="edge%d%d" % (h, g)) for g in range(G)] for h in range(HALVES)]
+        own = psum.tile([P, 512], F32, name="own")
+
+        def edge_pass(a, g, h, codes, scales):
+            for m in range(MT):
+                nc.tensor.matmul_mx(
+                    edge[h][g][:, m * H : (m + 1) * H],
+                    lhsT=w4[:, a, m * 2 * P : (m + 1) * 2 * P].bitcast(FP4X4),
+                    lhsT_scale=s4[:, a, m * P : (m + 1) * P],
+                    rhs=codes.bitcast(FP8X4),
+                    rhs_scale=scales,
+                    start=(a == 0 and m == 0),
+                    stop=(a == PASSES - 1 and m == MT - 1),
+                )
+
+        cq = []
+        d0 = [keep.tile([P, PACK, S], F32, name="d0%d" % g) for g in range(G)]
+        cw0 = weave4("cw0", cs[0][:], S)
+        for i in range(PACK):
+            for g in range(G):
+                gather(d0[g][:, i, :], 0, i, g, 0, S)
+            if i == 1:
+                cq.append(quantise("c0", cw0, S))
+        dw0 = [weave4("dw0%d" % g, d0[g][:], S) for g in range(G)]
+        cw1 = weave4("cw1", cs[1][:], S)
+
+        lo = [keep.tile([P, 2, S], F32, name="lo%d" % g) for g in range(G)]
+        hi = [[keep.tile([P, 2, H], F32, name="hi%d%d" % (h, g)) for g in range(G)] for h in range(HALVES)]
+        dw1 = [[keep.tile([P, H, PACK], BF16, name="dw1%d%d" % (h, g), align_bytes=64) for g in range(G)] for h in range(HALVES)]
+        for g in range(G):
+            gather(lo[g][:, 0, :], 1, 0, g, 0, S)
+        for g in range(G):
+            gather(lo[g][:, 1, :], 1, 1, g, 0, S)
+            for h in range(HALVES):
+                nc.scalar.copy(dw1[h][g][:, :, 0:2], lo[g][:, :, h * H : (h + 1) * H].rearrange("p t j -> p j t"))
+        for g in range(G):
+            codes, scales = quantise("d0%d" % g, dw0[g], S)
+            for h in range(HALVES):
+                edge_pass(0, g, h, codes[:, h * H : (h + 1) * H], scales[:, h * H : (h + 1) * H])
+        cq.append(quantise("c1", cw1, S))
+        for h in range(HALVES):
+            for g in range(G):
+                gather(hi[h][g][:, 0, :], 1, 2, g, h * H, H)
+        for h in range(HALVES):
+            for g in range(G):
+                gather(hi[h][g][:, 1, :], 1, 3, g, h * H, H)
+                nc.scalar.copy(dw1[h][g][:, :, 2:4], hi[h][g][:].rearrange("p t j -> p j t"))
+
+        for m in range(MT):
+            for a in range(PASSES):
+                nc.tensor.matmul_mx(
+                    own[:, m * S : (m + 1) * S],
+                    lhsT=w8[:, a, m * 4 * P : (m + 1) * 4 * P].bitcast(FP8X4),
+                    lhsT_scale=s8[:, a, m * P : (m + 1) * P],
+                    rhs=cq[a][0][:].bitcast(FP8X4),
+                    rhs_scale=cq[a][1][:],
+                    start=(a == 0),
+                    stop=(a == PASSES - 1),
+                )
+
+        first = []
+        for h in range(HALVES):
+            for g in range(G):
+                codes, scales = quantise("d1%d%d" % (h, g), dw1[h][g], H)
+                edge_pass(1, g, h, codes[:], scales[:])
+            held = keep.tile([P, MT * H], F32, name="first%d" % h)
+            nc.scalar.copy(held[:], edge[h][0][:, 0 : MT * H])
+            first.append(held)
+
+        out_rows = out.rearrange("(m p) j -> p m j", p=P)
+        for h in range(HALVES):
+            top = keep.tile([P, MT * H], F32, name="top%d" % h)
+            res = keep.tile([P, MT, H], F32, name="res%d" % h)
+            nc.vector.tensor_tensor(top[:], edge[h][1][:, 0 : MT * H], first[h][:], ALU.max)
+            for m in range(MT):
+                nc.vector.scalar_tensor_tensor(
+                    res[:, m, :],
+                    top[:, m * H : (m + 1) * H],
+                    bias[:, m : m + 1],
+                    own[:, m * S + h * H : m * S + (h + 1) * H],
+                    ALU.add,
+                    ALU.add,
+                )
+            nc.sync.dma_start(out_rows[:, :, h * H : (h + 1) * H], res[:])

@@ -34,30 +34,17 @@ def tile_list_edge_bias_kernel(tc, xT, c, w4_words, w4_scales, w8_words, w8_scal
         nc.sync.dma_start(offsets[:], offs)
 
         x_rows = xT.rearrange("(a p i) t -> a i p t", p=P, i=PACK)
-        c_rows = c.rearrange("(a p i) j -> a p i j", p=P, i=PACK)
-        xs = [[keep.tile([P, T], F32, name="x%d%d" % (a, i)) for i in range(PACK)] for a in range(PASSES)]
-        cs = [keep.tile([P, PACK, S], F32, name="c%d" % a) for a in range(PASSES)]
+        c_rows = c.rearrange("(a p u s) j -> a u p s j", p=P, u=2, s=2)
+        xs = [[keep.tile([P, T], F32, name="x%d%d" % (a, i), tag="x%d%d" % (a, i), align_bytes=64) for i in range(PACK)] for a in range(PASSES)]
+        cs = [keep.tile([P, 2, 4, S], F32, name="c%d" % a) for a in range(PASSES)]
         w4 = keep.tile([P, PASSES, 2 * M], U8, name="w4", align_bytes=64)
         w8 = keep.tile([P, PASSES, 4 * M], U8, name="w8", align_bytes=64)
         s4 = keep.tile([P, PASSES, M], U8, name="s4", align_bytes=64)
         s8 = keep.tile([P, PASSES, M], U8, name="s8", align_bytes=64)
         bias = keep.tile([P, MT], F32, name="bias")
 
-        nc.sync.dma_start(cs[0][:, 0:1, :], c_rows[0][:, 0:1, :])
-        nc.sync.dma_start(xs[0][0][:], x_rows[0][0])
-        nc.sync.dma_start(cs[0][:, 1:PACK, :], c_rows[0][:, 1:PACK, :])
-        for i in range(1, PACK):
-            nc.sync.dma_start(xs[0][i][:], x_rows[0][i])
-        nc.sync.dma_start(cs[1][:], c_rows[1])
-        nc.sync.dma_start(w4[:].bitcast(I32), w4_words.rearrange("a p n -> p a n").bitcast(I32))
-        for i in range(PACK):
-            nc.sync.dma_start(xs[1][i][:], x_rows[1][i])
-        nc.sync.dma_start(w8[:].bitcast(I32), w8_words.rearrange("a p n i -> p a (n i)").bitcast(I32))
-        with nc.allow_non_contiguous_dma(reason="one bias value a partition"):
-            nc.sync.dma_start(bias[:], b.rearrange("(m p) -> p m", p=P))
-
-        for plane, src in ((s4, w4_scales), (s8, w8_scales)):
-            nc.gpsimd.memset(plane[:].bitcast(I32), 0)
+        for plane in (s4, s8):
+            nc.vector.memset(plane[:].bitcast(I32), 0)
         for plane, src in ((s4, w4_scales), (s8, w8_scales)):
             for q in range(4):
                 nc.gpsimd.dma_start(
@@ -65,72 +52,101 @@ def tile_list_edge_bias_kernel(tc, xT, c, w4_words, w4_scales, w8_words, w8_scal
                     src[:, 4 * q : 4 * q + 4, :].rearrange("a r n -> r a n").bitcast(I32),
                 )
 
-        def gather(dst, a, i, g, j0, n):
-            lo = (g * S + j0) // 16
-            nc.vector.tensor_tensor(dst, xs[a][i][:].indirect(offsets[:, lo : lo + n // 16]), cs[a][:, i, j0 : j0 + n], ALU.subtract)
+        def load_c(a, u):
+            nc.sync.dma_start(cs[a][:, u, 1:3, :], c_rows[a][u])
 
-        def weave4(name, src, n):
-            woven = keep.tile([P, n, PACK], BF16, name=name, align_bytes=64)
+        def load_x(a, i):
+            nc.sync.dma_start(xs[a][i][:], x_rows[a][i])
+
+        nc.sync.dma_start(cs[0][:, :, 1:3, :], c.rearrange("(a p u s) j -> a p u s j", p=P, u=2, s=2)[0])
+        load_x(0, 0)
+        load_x(0, 1)
+        load_c(1, 0)
+        load_x(0, 2)
+        load_c(1, 1)
+        load_x(0, 3)
+        load_x(1, 0)
+        load_x(1, 1)
+        nc.sync.dma_start(w4[:].bitcast(I32), w4_words.rearrange("a p n -> p a n").bitcast(I32))
+        load_x(1, 2)
+        nc.sync.dma_start(w8[:].bitcast(I32), w8_words.rearrange("a p n i -> p a (n i)").bitcast(I32))
+        load_x(1, 3)
+        with nc.allow_non_contiguous_dma(reason="one bias value a partition"):
+            nc.sync.dma_start(bias[:], b.rearrange("(m p) -> p m", p=P))
+
+        def gather_part(dst, a, i, lo, n):
+            u, s = divmod(i, 2)
+            j0 = lo % S
+            nc.vector.tensor_tensor(dst, xs[a][i][:].indirect(offsets[:, lo // 16 : (lo + n) // 16]), cs[a][:, u, 1 + s, j0 : j0 + n], ALU.subtract)
+
+        def gather_all(dst, a, i):
+            u, s = divmod(i, 2)
+            twice = cs[a][:, u, 2 * s : 2 * s + 2, :].rearrange("p g j -> p (g j)")
+            nc.vector.tensor_tensor(dst, xs[a][i][:].indirect(offsets[:]), twice, ALU.subtract)
+
+        def weave_c(a):
+            woven = keep.tile([P, S, PACK], BF16, name="cw%d" % a, align_bytes=64)
             nc.scalar.copy(
-                woven[:].rearrange("p (c e) t -> p c t e", e=4),
-                src.rearrange("p t (c e) -> p c t e", e=4),
+                woven[:].rearrange("p (c e) (u s) -> p c u s e", e=4, u=2),
+                cs[a][:, :, 1:3, :].rearrange("p u s (c e) -> p c u s e", e=4),
             )
             return woven
 
-        def quantise(name, woven, n):
-            codes = keep.tile([P, n], U32, name=name + "q", align_bytes=64)
+        def weave_pair(woven, pair, u, cols):
+            nc.scalar.copy(woven[:, cols, 2 * u : 2 * u + 2], pair[:, :, cols].rearrange("p s j -> p j s"))
+
+        def quantise(name, woven, n, after=None):
+            codes = keep.tile([P, n], U32, name=name + "q", tag=after or name + "q", align_bytes=64)
             scales = keep.tile([P, n], U8, name=name + "s", align_bytes=64)
-            nc.vector.quantize_mx(codes[:].bitcast(FP8X4), scales[:], woven[:].rearrange("p j t -> p (j t)"))
+            nc.vector.quantize_mx(codes[:].bitcast(FP8X4), scales[:], woven.rearrange("p j t -> p (j t)"))
             return codes, scales
 
-        edge = [[psum.tile([P, 512], F32, name="edge%d%d" % (h, g)) for g in range(G)] for h in range(HALVES)]
+        edge = [[psum.tile([P, 512], F32, name="edge%d%d" % (g, h)) for h in range(HALVES)] for g in range(G)]
+        last = psum.tile([P, 512], F32, name="last")
+
+        def edge_sum(g, h, m):
+            if (g, h, m) == (G - 1, HALVES - 1, MT - 1):
+                return last[:, 0:H]
+            return edge[g][h][:, m * H : (m + 1) * H]
         own = psum.tile([P, 512], F32, name="own")
 
         def edge_pass(a, g, h, codes, scales):
+            apart = (g, h) == (G - 1, HALVES - 1)
             for m in range(MT):
                 nc.tensor.matmul_mx(
-                    edge[h][g][:, m * H : (m + 1) * H],
+                    edge_sum(g, h, m),
                     lhsT=w4[:, a, m * 2 * P : (m + 1) * 2 * P].bitcast(FP4X4),
                     lhsT_scale=s4[:, a, m * P : (m + 1) * P],
                     rhs=codes.bitcast(FP8X4),
                     rhs_scale=scales,
-                    start=(a == 0 and m == 0),
-                    stop=(a == PASSES - 1 and m == MT - 1),
+                    start=(a == 0 and (m == 0 or apart)),
+                    stop=(a == PASSES - 1 and (m == MT - 1 or apart)),
                 )
 
+        every = slice(0, G * S)
+        d0 = keep.tile([P, PACK, G * S], F32, name="d0")
+        d1 = [keep.tile([P, 2, G * S], F32, name="d1%d" % u) for u in range(2)]
+        dw = [keep.tile([P, G * S, PACK], BF16, name="dw%d" % a, align_bytes=64) for a in range(PASSES)]
         cq = []
-        d0 = [keep.tile([P, PACK, S], F32, name="d0%d" % g) for g in range(G)]
-        cw0 = weave4("cw0", cs[0][:], S)
-        for i in range(PACK):
-            for g in range(G):
-                gather(d0[g][:, i, :], 0, i, g, 0, S)
-            if i == 1:
-                cq.append(quantise("c0", cw0, S))
-        dw0 = [weave4("dw0%d" % g, d0[g][:], S) for g in range(G)]
-        cw1 = weave4("cw1", cs[1][:], S)
 
-        lo = [keep.tile([P, 2, S], F32, name="lo%d" % g) for g in range(G)]
-        hi = [[keep.tile([P, 2, H], F32, name="hi%d%d" % (h, g)) for g in range(G)] for h in range(HALVES)]
-        dw1 = [[keep.tile([P, H, PACK], BF16, name="dw1%d%d" % (h, g), align_bytes=64) for g in range(G)] for h in range(HALVES)]
-        for g in range(G):
-            gather(lo[g][:, 0, :], 1, 0, g, 0, S)
-        for g in range(G):
-            gather(lo[g][:, 1, :], 1, 1, g, 0, S)
-            for h in range(HALVES):
-                nc.scalar.copy(dw1[h][g][:, :, 0:2], lo[g][:, :, h * H : (h + 1) * H].rearrange("p t j -> p j t"))
-        for g in range(G):
-            codes, scales = quantise("d0%d" % g, dw0[g], S)
-            for h in range(HALVES):
-                edge_pass(0, g, h, codes[:, h * H : (h + 1) * H], scales[:, h * H : (h + 1) * H])
-        cq.append(quantise("c1", cw1, S))
-        for h in range(HALVES):
-            for g in range(G):
-                gather(hi[h][g][:, 0, :], 1, 2, g, h * H, H)
-        for h in range(HALVES):
-            for g in range(G):
-                gather(hi[h][g][:, 1, :], 1, 3, g, h * H, H)
-                nc.scalar.copy(dw1[h][g][:, :, 2:4], hi[h][g][:].rearrange("p t j -> p j t"))
-
+        nc.vector.tensor_copy(cs[0][:, :, 0:4:3, :], cs[0][:, :, 1:3, :])
+        cw0 = weave_c(0)
+        gather_all(d0[:, 0, :], 0, 0)
+        cq.append(quantise("c0", cw0[:], S))
+        nc.scalar.copy(cs[1][:, 0, 0:4:3, :], cs[1][:, 0, 1:3, :])
+        gather_all(d0[:, 1, :], 0, 1)
+        gather_all(d0[:, 2, :], 0, 2)
+        cw1 = weave_c(1)
+        nc.scalar.copy(cs[1][:, 1, 0, :], cs[1][:, 1, 1, :])
+        gather_all(d0[:, 3, :], 0, 3)
+        nc.scalar.copy(
+            dw[0][:].rearrange("p (c e) t -> p c t e", e=4),
+            d0[:].rearrange("p t (c e) -> p c t e", e=4),
+        )
+        cq.append(quantise("c1", cw1[:], S))
+        gather_all(d1[0][:, 0, :], 1, 0)
+        gather_all(d1[0][:, 1, :], 1, 1)
+        weave_pair(dw[1], d1[0], 0, every)
         for m in range(MT):
             for a in range(PASSES):
                 nc.tensor.matmul_mx(
@@ -143,27 +159,45 @@ def tile_list_edge_bias_kernel(tc, xT, c, w4_words, w4_scales, w8_words, w8_scal
                     stop=(a == PASSES - 1),
                 )
 
+        codes, scales = quantise("d0", dw[0][:], G * S)
+        for g in range(G):
+            for h in range(HALVES):
+                cols = slice(g * S + h * H, g * S + (h + 1) * H)
+                edge_pass(0, g, h, codes[:, cols], scales[:, cols])
+        gather_all(d1[1][:, 0, :], 1, 2)
+
+        for g in range(G):
+            for h in range(HALVES):
+                cols = slice(g * S + h * H, g * S + (h + 1) * H)
+                gather_part(d1[1][:, 1, cols], 1, 3, cols.start, H)
+                weave_pair(dw[1], d1[1], 1, cols)
+
         first = []
-        for h in range(HALVES):
-            for g in range(G):
-                codes, scales = quantise("d1%d%d" % (h, g), dw1[h][g], H)
+        for g in range(G):
+            for h in range(HALVES):
+                cols = slice(g * S + h * H, g * S + (h + 1) * H)
+                codes, scales = quantise("d1%d%d" % (g, h), dw[1][:, cols, :], H)
                 edge_pass(1, g, h, codes[:], scales[:])
-            held = keep.tile([P, MT * H], F32, name="first%d" % h)
-            nc.scalar.copy(held[:], edge[h][0][:, 0 : MT * H])
-            first.append(held)
+                if g == 0:
+                    held = keep.tile([P, MT * H], F32, name="first%d" % h)
+                    nc.scalar.copy(held[:], edge[0][h][:, 0 : MT * H])
+                    first.append(held)
 
         out_rows = out.rearrange("(m p) j -> p m j", p=P)
-        for h in range(HALVES):
-            top = keep.tile([P, MT * H], F32, name="top%d" % h)
-            res = keep.tile([P, MT, H], F32, name="res%d" % h)
-            nc.vector.tensor_tensor(top[:], edge[h][1][:, 0 : MT * H], first[h][:], ALU.max)
-            for m in range(MT):
-                nc.vector.scalar_tensor_tensor(
-                    res[:, m, :],
-                    top[:, m * H : (m + 1) * H],
-                    bias[:, m : m + 1],
-                    own[:, m * S + h * H : m * S + (h + 1) * H],
-                    ALU.add,
-                    ALU.add,
-                )
-            nc.sync.dma_start(out_rows[:, :, h * H : (h + 1) * H], res[:])
+
+        def finish(res, top, h, m):
+            nc.vector.scalar_tensor_tensor(res, top, bias[:, m : m + 1], own[:, m * S + h * H : m * S + (h + 1) * H], ALU.add, ALU.add)
+
+        top = keep.tile([P, MT * H], F32, name="top0")
+        res = keep.tile([P, MT, H], F32, name="res0")
+        nc.vector.tensor_tensor(top[:], edge[1][0][:, 0 : MT * H], first[0][:], ALU.max)
+        for m in range(MT):
+            finish(res[:, m, :], top[:, m * H : (m + 1) * H], 0, m)
+        nc.sync.dma_start(out_rows[:, :, 0:H], res[:])
+        tops = [keep.tile([P, H], F32, name="top1%d" % m) for m in range(MT)]
+        for m in range(MT):
+            nc.vector.tensor_tensor(tops[m][:], edge_sum(1, 1, m), first[1][:, m * H : (m + 1) * H], ALU.max)
+        for m, queue in enumerate((nc.scalar, nc.sync)):
+            res = keep.tile([P, H], F32, name="res1%d" % m)
+            finish(res[:], tops[m][:], 1, m)
+            queue.dma_start(out_rows[:, m, H : 2 * H], res[:])

from contextlib import ExitStack

import concourse.mybir as mybir

G, K, M, T, S = 2, 1024, 256, 1024, 256
FLOPS = 2 * K * M * S * (G + 1)

F32 = mybir.dt.float32
BF16 = mybir.dt.bfloat16
I32 = mybir.dt.int32
U32 = mybir.dt.uint32
U16 = mybir.dt.uint16
U8 = mybir.dt.uint8
FP8X4 = mybir.dt.float8_e4m3fn_x4
FP4X4 = mybir.dt.float4_e2m1fn_x4
ALU = mybir.AluOpType

P = 128
PACK = 4
KP = P * PACK
PASSES = K // KP
MT = M // P
H = 128
HALVES = S // H


def tile_list_edge_bias_kernel(tc, xT, c, w4_words, w4_scales, w8_words, w8_scales, b, offs, out):
    nc = tc.nc
    with ExitStack() as ctx:
        keep = ctx.enter_context(tc.tile_pool(name="keep", bufs=1))
        psum = ctx.enter_context(tc.psum_pool(name="psum", bufs=1))

        offsets = keep.tile([P, G * S // 16], U16, name="offsets")
        nc.sync.dma_start(offsets[:], offs)

        x_rows = xT.rearrange("(a p i) t -> a i p t", p=P, i=PACK)
        c_rows = c.rearrange("(a p u s) j -> a u p s j", p=P, u=2, s=2)
        xs = [[keep.tile([P, T], F32, name="x%d%d" % (a, i), tag="x%d%d" % (a, i), align_bytes=64) for i in range(PACK)] for a in range(PASSES)]
        cs = [keep.tile([P, 2, 4, S], F32, name="c%d" % a) for a in range(PASSES)]
        w4 = keep.tile([P, PASSES, 2 * M], U8, name="w4", align_bytes=64)
        w8 = keep.tile([P, PASSES, 4 * M], U8, name="w8", align_bytes=64)
        s4 = keep.tile([P, PASSES, M], U8, name="s4", align_bytes=64)
        s8 = keep.tile([P, PASSES, M], U8, name="s8", align_bytes=64)
        bias = keep.tile([P, MT], F32, name="bias")

        for plane in (s4, s8):
            nc.vector.memset(plane[:].bitcast(I32), 0)
        for plane, src in ((s4, w4_scales), (s8, w8_scales)):
            for q in range(4):
                nc.gpsimd.dma_start(
                    plane[32 * q : 32 * q + 4].bitcast(I32),
                    src[:, 4 * q : 4 * q + 4, :].rearrange("a r n -> r a n").bitcast(I32),
                )

        def load_c(a, u):
            nc.sync.dma_start(cs[a][:, u, 1:3, :], c_rows[a][u])

        def load_x(a, i):
            nc.sync.dma_start(xs[a][i][:], x_rows[a][i])

        nc.sync.dma_start(cs[0][:, :, 1:3, :], c.rearrange("(a p u s) j -> a p u s j", p=P, u=2, s=2)[0])
        load_x(0, 0)
        load_x(0, 1)
        load_c(1, 0)
        load_x(0, 2)
        load_c(1, 1)
        load_x(0, 3)
        load_x(1, 0)
        load_x(1, 1)
        nc.sync.dma_start(w4[:].bitcast(I32), w4_words.rearrange("a p n -> p a n").bitcast(I32))
        load_x(1, 2)
        nc.sync.dma_start(w8[:].bitcast(I32), w8_words.rearrange("a p n i -> p a (n i)").bitcast(I32))
        load_x(1, 3)
        with nc.allow_non_contiguous_dma(reason="one bias value a partition"):
            nc.sync.dma_start(bias[:], b.rearrange("(m p) -> p m", p=P))

        def gather_part(dst, a, i, lo, n):
            u, s = divmod(i, 2)
            j0 = lo % S
            nc.vector.tensor_tensor(dst, xs[a][i][:].indirect(offsets[:, lo // 16 : (lo + n) // 16]), cs[a][:, u, 1 + s, j0 : j0 + n], ALU.subtract)

        def gather_all(dst, a, i):
            u, s = divmod(i, 2)
            twice = cs[a][:, u, 2 * s : 2 * s + 2, :].rearrange("p g j -> p (g j)")
            nc.vector.tensor_tensor(dst, xs[a][i][:].indirect(offsets[:]), twice, ALU.subtract)

        def weave_c(a):
            woven = keep.tile([P, S, PACK], BF16, name="cw%d" % a, align_bytes=64)
            nc.scalar.copy(
                woven[:].rearrange("p (c e) (u s) -> p c u s e", e=4, u=2),
                cs[a][:, :, 1:3, :].rearrange("p u s (c e) -> p c u s e", e=4),
            )
            return woven

        def weave_pair(woven, pair, u, cols):
            nc.scalar.copy(woven[:, cols, 2 * u : 2 * u + 2], pair[:, :, cols].rearrange("p s j -> p j s"))

        def quantise(name, woven, n, after=None):
            codes = keep.tile([P, n], U32, name=name + "q", tag=after or name + "q", align_bytes=64)
            scales = keep.tile([P, n], U8, name=name + "s", align_bytes=64)
            nc.vector.quantize_mx(codes[:].bitcast(FP8X4), scales[:], woven.rearrange("p j t -> p (j t)"))
            return codes, scales

        edge = [[psum.tile([P, 512], F32, name="edge%d%d" % (g, h)) for h in range(HALVES)] for g in range(G)]
        last = psum.tile([P, 512], F32, name="last")

        def edge_sum(g, h, m):
            if (g, h, m) == (G - 1, HALVES - 1, MT - 1):
                return last[:, 0:H]
            return edge[g][h][:, m * H : (m + 1) * H]
        own = psum.tile([P, 512], F32, name="own")

        def edge_pass(a, g, h, codes, scales):
            apart = (g, h) == (G - 1, HALVES - 1)
            for m in range(MT):
                nc.tensor.matmul_mx(
                    edge_sum(g, h, m),
                    lhsT=w4[:, a, m * 2 * P : (m + 1) * 2 * P].bitcast(FP4X4),
                    lhsT_scale=s4[:, a, m * P : (m + 1) * P],
                    rhs=codes.bitcast(FP8X4),
                    rhs_scale=scales,
                    start=(a == 0 and (m == 0 or apart)),
                    stop=(a == PASSES - 1 and (m == MT - 1 or apart)),
                )

        every = slice(0, G * S)
        d0 = keep.tile([P, PACK, G * S], F32, name="d0")
        d1 = [keep.tile([P, 2, G * S], F32, name="d1%d" % u) for u in range(2)]
        dw = [keep.tile([P, G * S, PACK], BF16, name="dw%d" % a, align_bytes=64) for a in range(PASSES)]
        cq = []

        nc.vector.tensor_copy(cs[0][:, :, 0:4:3, :], cs[0][:, :, 1:3, :])
        cw0 = weave_c(0)
        gather_all(d0[:, 0, :], 0, 0)
        cq.append(quantise("c0", cw0[:], S))
        nc.scalar.copy(cs[1][:, 0, 0:4:3, :], cs[1][:, 0, 1:3, :])
        gather_all(d0[:, 1, :], 0, 1)
        gather_all(d0[:, 2, :], 0, 2)
        cw1 = weave_c(1)
        nc.scalar.copy(cs[1][:, 1, 0, :], cs[1][:, 1, 1, :])
        gather_all(d0[:, 3, :], 0, 3)
        nc.scalar.copy(
            dw[0][:].rearrange("p (c e) t -> p c t e", e=4),
            d0[:].rearrange("p t (c e) -> p c t e", e=4),
        )
        cq.append(quantise("c1", cw1[:], S))
        gather_all(d1[0][:, 0, :], 1, 0)
        gather_all(d1[0][:, 1, :], 1, 1)
        weave_pair(dw[1], d1[0], 0, every)
        for m in range(MT):
            for a in range(PASSES):
                nc.tensor.matmul_mx(
                    own[:, m * S : (m + 1) * S],
                    lhsT=w8[:, a, m * 4 * P : (m + 1) * 4 * P].bitcast(FP8X4),
                    lhsT_scale=s8[:, a, m * P : (m + 1) * P],
                    rhs=cq[a][0][:].bitcast(FP8X4),
                    rhs_scale=cq[a][1][:],
                    start=(a == 0),
                    stop=(a == PASSES - 1),
                )

        codes, scales = quantise("d0", dw[0][:], G * S)
        for g in range(G):
            for h in range(HALVES):
                cols = slice(g * S + h * H, g * S + (h + 1) * H)
                edge_pass(0, g, h, codes[:, cols], scales[:, cols])
        gather_all(d1[1][:, 0, :], 1, 2)

        for g in range(G):
            for h in range(HALVES):
                cols = slice(g * S + h * H, g * S + (h + 1) * H)
                gather_part(d1[1][:, 1, cols], 1, 3, cols.start, H)
                weave_pair(dw[1], d1[1], 1, cols)

        first = []
        for g in range(G):
            for h in range(HALVES):
                cols = slice(g * S + h * H, g * S + (h + 1) * H)
                codes, scales = quantise("d1%d%d" % (g, h), dw[1][:, cols, :], H)
                edge_pass(1, g, h, codes[:], scales[:])
                if g == 0:
                    held = keep.tile([P, MT * H], F32, name="first%d" % h)
                    nc.scalar.copy(held[:], edge[0][h][:, 0 : MT * H])
                    first.append(held)

        out_rows = out.rearrange("(m p) j -> p m j", p=P)

        def finish(res, top, h, m):
            nc.vector.scalar_tensor_tensor(res, top, bias[:, m : m + 1], own[:, m * S + h * H : m * S + (h + 1) * H], ALU.add, ALU.add)

        top = keep.tile([P, MT * H], F32, name="top0")
        res = keep.tile([P, MT, H], F32, name="res0")
        nc.vector.tensor_tensor(top[:], edge[1][0][:, 0 : MT * H], first[0][:], ALU.max)
        for m in range(MT):
            finish(res[:, m, :], top[:, m * H : (m + 1) * H], 0, m)
        nc.sync.dma_start(out_rows[:, :, 0:H], res[:])
        tops = [keep.tile([P, H], F32, name="top1%d" % m) for m in range(MT)]
        for m in range(MT):
            nc.vector.tensor_tensor(tops[m][:], edge_sum(1, 1, m), first[1][:, m * H : (m + 1) * H], ALU.max)
        for m, queue in enumerate((nc.scalar, nc.sync)):
            res = keep.tile([P, H], F32, name="res1%d" % m)
            finish(res[:], tops[m][:], 1, m)
            queue.dma_start(out_rows[:, m, H : 2 * H], res[:])
